import numpy as np
CORES = [3,11,19,27,35,43,51,59,67,75,83,91]
N = 12
def setup_inputs(rng):
    return {"x": rng.standard_normal((N, 128, 128), dtype=np.float32)}
def reference(x):
    g = np.concatenate(list(x), axis=1)
    return {"y": np.broadcast_to(g, (N,) + g.shape)}

@@ -1,0 +1,86 @@
+from concourse.bass import DstId, RemoteDMATransfer
+
+B = 128
+GRP = 4
+NG = 3
+
+SCRATCH = {
+    "land": ("sbuf", [128, 12 * B], "float32"),
+    "xd": ("dram", [128, B], "float32"),
+}
+SEMAPHORES = ["ld_s", "ld_d", "got", "sent", "arr0", "arr1", "arr2", "stored"]
+
+RANK_CORE = 3
+PLAN = {
+    3: [(0, [(0, 1), (0, 3), (0, 2)])],
+    2: [(1, [(-1, 1)]), (2, [(1, 0)])],
+    6: [(1, [(-1, 3)]), (2, [(1, 1)])],
+    7: [(2, [(1, 3), (1, 2)])],
+    0: [(1, [(-1, 0)])],
+    4: [(1, [(-1, 2)])],
+}
+HELPERS = [2, 6, 7, 0, 4]
+
+
+def dest_chip(s, d, k):
+    return GRP * ((s // GRP + d) % NG) + ((s % GRP) ^ k)
+
+
+def send_blocks(g, T, topo, s, calls):
+    arr = [T.sem.arr0, T.sem.arr1, T.sem.arr2]
+    n = 0
+    for sem, classes in calls:
+        ids = []
+        for d, k in classes:
+            rid, pid, _se = topo.addr(8 * dest_chip(s, d, k) + RANK_CORE)
+            ids.append(DstId(rid=rid, pnc=pid))
+        g.remote_dma_fused(
+            [RemoteDMATransfer(dst_ids=ids, dma_engine_mask=0x00FF, remote_sem=arr[sem],
+                               srcs=[T.xd[:]], dsts=[T.land[:, s * B:(s + 1) * B] for _ in ids])],
+            local_sem=T.sem.sent)
+        n += 8
+    return n
+
+
+def rank_program(g, core, T, topo):
+    s, k = divmod(core, 8)
+    if k not in PLAN:
+        return
+
+    if k != RANK_CORE:
+        g.wait_ge(T.sem.got, 16)
+        n = send_blocks(g, T, topo, s, PLAN[k])
+        g.wait_ge(T.sem.sent, n)
+        return
+
+    g.scalar.dma_start(T.xd[:], T.x[:]).then_inc(T.sem.ld_d, 16)
+    g.sync.dma_start(T.land[:, s * B:(s + 1) * B], T.x[:]).then_inc(T.sem.ld_s, 16)
+
+    g.wait_ge(T.sem.ld_d, 16)
+    ids = []
+    for h in HELPERS:
+        rid, pid, _se = topo.addr(8 * s + h)
+        ids.append(DstId(rid=rid, pnc=pid))
+    g.remote_dma_fused(
+        [RemoteDMATransfer(dst_ids=ids, dma_engine_mask=0xFFFF, remote_sem=T.sem.got,
+                           srcs=[T.xd[:]], dsts=[T.xd[:] for _ in ids])],
+        local_sem=T.sem.sent)
+    n = 16 + send_blocks(g, T, topo, s, PLAN[RANK_CORE])
+
+    a = s // GRP
+    W = GRP * B
+
+    def cols(grp):
+        return slice(grp * W, (grp + 1) * W)
+
+    g0, g1, g2 = a, (a + 1) % NG, (a - 1) % NG
+    g.sync.wait_ge(T.sem.ld_s, 16)
+    g.sync.wait_ge(T.sem.arr0, 24)
+    g.sync.dma_start(T.y[:, cols(g0)], T.land[:, cols(g0)]).then_inc(T.sem.stored, 16)
+    g.scalar.wait_ge(T.sem.arr1, 32)
+    g.scalar.dma_start(T.y[:, cols(g1)], T.land[:, cols(g1)]).then_inc(T.sem.stored, 16)
+    g.sync.wait_ge(T.sem.arr2, 32)
+    g.sync.dma_start(T.y[:, cols(g2)], T.land[:, cols(g2)]).then_inc(T.sem.stored, 16)
+
+    g.wait_ge(T.sem.sent, n)
+    g.wait_ge(T.sem.stored, 48)

@@ -1,86 +1,95 @@
 from concourse.bass import DstId, RemoteDMATransfer
 
 B = 128
-GRP = 4
-NG = 3
+NP = 6
+R = 3
+RELAY = {1: 2, 2: 6, 3: 7}
+LO, HI = 0x00FF, 0xFF00
 
 SCRATCH = {
     "land": ("sbuf", [128, 12 * B], "float32"),
     "xd": ("dram", [128, B], "float32"),
+    "rl": ("dram", [128, B], "float32"),
 }
-SEMAPHORES = ["ld_s", "ld_d", "got", "sent", "arr0", "arr1", "arr2", "stored"]
-
-RANK_CORE = 3
-PLAN = {
-    3: [(0, [(0, 1), (0, 3), (0, 2)])],
-    2: [(1, [(-1, 1)]), (2, [(1, 0)])],
-    6: [(1, [(-1, 3)]), (2, [(1, 1)])],
-    7: [(2, [(1, 3), (1, 2)])],
-    0: [(1, [(-1, 0)])],
-    4: [(1, [(-1, 2)])],
-}
-HELPERS = [2, 6, 7, 0, 4]
+SEMAPHORES = ["ld_s", "ld_d", "got", "rin", "sent", "a_own", "a_r1", "a_r2", "a_r3", "a_d1", "a_d2", "stored"]
 
 
-def dest_chip(s, d, k):
-    return GRP * ((s // GRP + d) % NG) + ((s % GRP) ^ k)
-
-
-def send_blocks(g, T, topo, s, calls):
-    arr = [T.sem.arr0, T.sem.arr1, T.sem.arr2]
-    n = 0
-    for sem, classes in calls:
-        ids = []
-        for d, k in classes:
-            rid, pid, _se = topo.addr(8 * dest_chip(s, d, k) + RANK_CORE)
-            ids.append(DstId(rid=rid, pnc=pid))
-        g.remote_dma_fused(
-            [RemoteDMATransfer(dst_ids=ids, dma_engine_mask=0x00FF, remote_sem=arr[sem],
-                               srcs=[T.xd[:]], dsts=[T.land[:, s * B:(s + 1) * B] for _ in ids])],
-            local_sem=T.sem.sent)
-        n += 8
-    return n
+def chip_at(c, o, cross):
+    return 2 * ((c // 2 + o) % NP) + ((c & 1) ^ (1 if cross else 0))
 
 
 def rank_program(g, core, T, topo):
-    s, k = divmod(core, 8)
-    if k not in PLAN:
-        return
+    c, k = divmod(core, 8)
 
-    if k != RANK_CORE:
-        g.wait_ge(T.sem.got, 16)
-        n = send_blocks(g, T, topo, s, PLAN[k])
+    def dst(core_):
+        rid, pid, _se = topo.addr(core_)
+        return DstId(rid=rid, pnc=pid)
+
+    def block(s):
+        return T.land[:, s * B:(s + 1) * B]
+
+    def to_land(src, s, chips, mask, sem):
+        return RemoteDMATransfer(dst_ids=[dst(8 * j + R) for j in chips], dma_engine_mask=mask, remote_sem=sem,
+                                 srcs=[src], dsts=[block(s) for _ in chips])
+
+    def relay(o):
+        s = chip_at(c, -o, False)
+        sem = T.sem["a_r%d" % o]
+        g.wait_ge(T.sem.rin, 8)
+        g.remote_dma_fused([to_land(T.rl[:], s, [c ^ 1], LO, sem), to_land(T.rl[:], s, [c], HI, sem)],
+                           local_sem=T.sem.sent)
+        return 16
+
+    if k in (2, 6):
+        n = relay(1 if k == 2 else 2)
         g.wait_ge(T.sem.sent, n)
-        return
+    elif k == 7:
+        g.wait_ge(T.sem.got, 8)
+        g.remote_dma_fused([to_land(T.xd[:], c, [chip_at(c, 4, True)], LO, T.sem.a_d2)], local_sem=T.sem.sent)
+        n = 8 + relay(3)
+        g.wait_ge(T.sem.sent, n)
+    elif k == 4:
+        g.wait_ge(T.sem.got, 8)
+        g.remote_dma_fused([to_land(T.xd[:], c, [chip_at(c, 5, False)], LO, T.sem.a_d1)], local_sem=T.sem.sent)
+        g.remote_dma_fused([to_land(T.xd[:], c, [chip_at(c, 4, False)], LO, T.sem.a_d2)], local_sem=T.sem.sent)
+        g.wait_ge(T.sem.sent, 16)
+    elif k == R:
+        g.scalar.dma_start(T.xd[:], T.x[:]).then_inc(T.sem.ld_d, 16)
+        g.sync.dma_start(block(c), T.x[:]).then_inc(T.sem.ld_s, 16)
 
-    g.scalar.dma_start(T.xd[:], T.x[:]).then_inc(T.sem.ld_d, 16)
-    g.sync.dma_start(T.land[:, s * B:(s + 1) * B], T.x[:]).then_inc(T.sem.ld_s, 16)
+        g.wait_ge(T.sem.ld_d, 16)
+        g.remote_dma_fused(
+            [RemoteDMATransfer(dst_ids=[dst(8 * chip_at(c, o, False) + RELAY[o]) for o in (1, 2, 3)],
+                               dma_engine_mask=LO, remote_sem=T.sem.rin,
+                               srcs=[T.xd[:]], dsts=[T.rl[:] for _ in range(3)]),
+             RemoteDMATransfer(dst_ids=[dst(8 * c + 4), dst(8 * c + 7)],
+                               dma_engine_mask=HI, remote_sem=T.sem.got,
+                               srcs=[T.xd[:]], dsts=[T.xd[:] for _ in range(2)])],
+            local_sem=T.sem.sent)
+        g.remote_dma_fused(
+            [to_land(T.xd[:], c, [c ^ 1], 0x000F, T.sem.a_own),
+             to_land(T.xd[:], c, [chip_at(c, 5, True)], 0x00F0, T.sem.a_d1)],
+            local_sem=T.sem.sent)
 
-    g.wait_ge(T.sem.ld_d, 16)
-    ids = []
-    for h in HELPERS:
-        rid, pid, _se = topo.addr(8 * s + h)
-        ids.append(DstId(rid=rid, pnc=pid))
-    g.remote_dma_fused(
-        [RemoteDMATransfer(dst_ids=ids, dma_engine_mask=0xFFFF, remote_sem=T.sem.got,
-                           srcs=[T.xd[:]], dsts=[T.xd[:] for _ in ids])],
-        local_sem=T.sem.sent)
-    n = 16 + send_blocks(g, T, topo, s, PLAN[RANK_CORE])
+        p = c // 2
 
-    a = s // GRP
-    W = GRP * B
+        def store(q, o):
+            lo = 2 * B * ((p + o) % NP)
+            q.dma_start(T.y[:, lo:lo + 2 * B], T.land[:, lo:lo + 2 * B]).then_inc(T.sem.stored, 16)
 
-    def cols(grp):
-        return slice(grp * W, (grp + 1) * W)
+        g.sync.wait_ge(T.sem.ld_s, 16)
+        g.sync.wait_ge(T.sem.a_own, 4)
+        store(g.sync, 0)
+        g.sync.wait_ge(T.sem.a_r1, 16)
+        store(g.sync, -1)
+        g.sync.wait_ge(T.sem.a_r2, 16)
+        store(g.sync, -2)
+        g.sync.wait_ge(T.sem.a_r3, 16)
+        store(g.sync, -3)
+        g.scalar.wait_ge(T.sem.a_d1, 12)
+        store(g.scalar, 1)
+        g.scalar.wait_ge(T.sem.a_d2, 16)
+        store(g.scalar, 2)
 
-    g0, g1, g2 = a, (a + 1) % NG, (a - 1) % NG
-    g.sync.wait_ge(T.sem.ld_s, 16)
-    g.sync.wait_ge(T.sem.arr0, 24)
-    g.sync.dma_start(T.y[:, cols(g0)], T.land[:, cols(g0)]).then_inc(T.sem.stored, 16)
-    g.scalar.wait_ge(T.sem.arr1, 32)
-    g.scalar.dma_start(T.y[:, cols(g1)], T.land[:, cols(g1)]).then_inc(T.sem.stored, 16)
-    g.sync.wait_ge(T.sem.arr2, 32)
-    g.sync.dma_start(T.y[:, cols(g2)], T.land[:, cols(g2)]).then_inc(T.sem.stored, 16)
-
-    g.wait_ge(T.sem.sent, n)
-    g.wait_ge(T.sem.stored, 48)
+        g.wait_ge(T.sem.sent, 24)
+        g.wait_ge(T.sem.stored, 96)

from concourse.bass import DstId, RemoteDMATransfer

B = 128
NP = 6
R = 3
RELAY = {1: 2, 2: 6, 3: 7}
LO, HI = 0x00FF, 0xFF00

SCRATCH = {
    "land": ("sbuf", [128, 12 * B], "float32"),
    "xd": ("dram", [128, B], "float32"),
    "rl": ("dram", [128, B], "float32"),
}
SEMAPHORES = ["ld_s", "ld_d", "got", "rin", "sent", "a_own", "a_r1", "a_r2", "a_r3", "a_d1", "a_d2", "stored"]


def chip_at(c, o, cross):
    return 2 * ((c // 2 + o) % NP) + ((c & 1) ^ (1 if cross else 0))


def rank_program(g, core, T, topo):
    c, k = divmod(core, 8)

    def dst(core_):
        rid, pid, _se = topo.addr(core_)
        return DstId(rid=rid, pnc=pid)

    def block(s):
        return T.land[:, s * B:(s + 1) * B]

    def to_land(src, s, chips, mask, sem):
        return RemoteDMATransfer(dst_ids=[dst(8 * j + R) for j in chips], dma_engine_mask=mask, remote_sem=sem,
                                 srcs=[src], dsts=[block(s) for _ in chips])

    def relay(o):
        s = chip_at(c, -o, False)
        sem = T.sem["a_r%d" % o]
        g.wait_ge(T.sem.rin, 8)
        g.remote_dma_fused([to_land(T.rl[:], s, [c ^ 1], LO, sem), to_land(T.rl[:], s, [c], HI, sem)],
                           local_sem=T.sem.sent)
        return 16

    if k in (2, 6):
        n = relay(1 if k == 2 else 2)
        g.wait_ge(T.sem.sent, n)
    elif k == 7:
        g.wait_ge(T.sem.got, 8)
        g.remote_dma_fused([to_land(T.xd[:], c, [chip_at(c, 4, True)], LO, T.sem.a_d2)], local_sem=T.sem.sent)
        n = 8 + relay(3)
        g.wait_ge(T.sem.sent, n)
    elif k == 4:
        g.wait_ge(T.sem.got, 8)
        g.remote_dma_fused([to_land(T.xd[:], c, [chip_at(c, 5, False)], LO, T.sem.a_d1)], local_sem=T.sem.sent)
        g.remote_dma_fused([to_land(T.xd[:], c, [chip_at(c, 4, False)], LO, T.sem.a_d2)], local_sem=T.sem.sent)
        g.wait_ge(T.sem.sent, 16)
    elif k == R:
        g.scalar.dma_start(T.xd[:], T.x[:]).then_inc(T.sem.ld_d, 16)
        g.sync.dma_start(block(c), T.x[:]).then_inc(T.sem.ld_s, 16)

        g.wait_ge(T.sem.ld_d, 16)
        g.remote_dma_fused(
            [RemoteDMATransfer(dst_ids=[dst(8 * chip_at(c, o, False) + RELAY[o]) for o in (1, 2, 3)],
                               dma_engine_mask=LO, remote_sem=T.sem.rin,
                               srcs=[T.xd[:]], dsts=[T.rl[:] for _ in range(3)]),
             RemoteDMATransfer(dst_ids=[dst(8 * c + 4), dst(8 * c + 7)],
                               dma_engine_mask=HI, remote_sem=T.sem.got,
                               srcs=[T.xd[:]], dsts=[T.xd[:] for _ in range(2)])],
            local_sem=T.sem.sent)
        g.remote_dma_fused(
            [to_land(T.xd[:], c, [c ^ 1], 0x000F, T.sem.a_own),
             to_land(T.xd[:], c, [chip_at(c, 5, True)], 0x00F0, T.sem.a_d1)],
            local_sem=T.sem.sent)

        p = c // 2

        def store(q, o):
            lo = 2 * B * ((p + o) % NP)
            q.dma_start(T.y[:, lo:lo + 2 * B], T.land[:, lo:lo + 2 * B]).then_inc(T.sem.stored, 16)

        g.sync.wait_ge(T.sem.ld_s, 16)
        g.sync.wait_ge(T.sem.a_own, 4)
        store(g.sync, 0)
        g.sync.wait_ge(T.sem.a_r1, 16)
        store(g.sync, -1)
        g.sync.wait_ge(T.sem.a_r2, 16)
        store(g.sync, -2)
        g.sync.wait_ge(T.sem.a_r3, 16)
        store(g.sync, -3)
        g.scalar.wait_ge(T.sem.a_d1, 12)
        store(g.scalar, 1)
        g.scalar.wait_ge(T.sem.a_d2, 16)
        store(g.scalar, 2)

        g.wait_ge(T.sem.sent, 24)
        g.wait_ge(T.sem.stored, 96)
